import numpy as np
import ml_dtypes


def mxq(x, axis, fmt="e4m3"):
    dtype, down = {"e4m3": (ml_dtypes.float8_e4m3fn, 7), "e5m2": (ml_dtypes.float8_e5m2, 14)}[fmt]
    v = np.moveaxis(np.asarray(x, np.float32).astype(ml_dtypes.bfloat16).astype(np.float64), axis, -1)
    blocks = v.reshape(v.shape[:-1] + (-1, 32))
    amax = np.abs(blocks).max(-1, keepdims=True)
    byte = np.maximum(np.where(amax > 0, np.frexp(amax)[1] - 1 + 127, 0) - down, 1)
    scale = np.exp2(byte - 127.0)
    codes = (blocks / scale).astype(np.float32).astype(dtype).astype(np.float64)
    return np.moveaxis((codes * scale).reshape(v.shape), -1, axis)


WIDE = False


def mx_kscale(k):
    if not WIDE:
        return np.ones(k)
    levels = np.array([10, -10, 5, -5, 0])
    if k % 512:
        return np.exp2(np.random.permutation(np.resize(levels, k // 32))).repeat(32)
    a = np.empty((k // 512, 16))
    for p in range(k // 512):
        a[p, :8] = np.random.permutation(np.resize(levels, 8))
        for g in range(8):
            far = levels[np.abs(levels - a[p, g]) >= 10]
            a[p, g + 8] = far[np.random.randint(len(far))]
    return np.exp2(a.ravel()).repeat(32)


def f64(x):
    return np.asarray(x).astype(np.float64)


def striped(idx):
    return np.tile(np.asarray(idx).reshape(-1, 16).T, (8, 1)).astype(np.uint16)


def unstriped(offs):
    return offs[:16].T.reshape(-1).astype(np.int64)


O, G, K, T, D, M = 3, 256, 8, 2048, 1024, 128


def setup_inputs():
    n = np.random.standard_normal
    s = mx_kscale(D)[:, None]
    grid = lambda x: np.round(x * 32) / 32
    part = np.random.randint(1, 128 // K, (O, G, K)) / 64.0
    return {
        "xT": (grid(n((D, T))) * s).astype(np.float32),
        "w": (n((O, D, M)) / np.sqrt(O * D) / s).astype(np.float32),
        "part": np.tile(part.reshape(-1), (128, 1)).astype(np.float32),
        "offs": striped(np.random.randint(0, T, O * G * K)),
    }


def reference(xT, w, part, offs):
    x = f64(xT)[:, unstriped(offs)] * f64(part)[:1]
    e = mxq(x.reshape(D, O, G, K).sum(-1), 0, "e4m3")
    wq = mxq(f64(w), 1, "e4m3")
    y = sum(wq[o].T @ e[:, o] for o in range(O))
    return y

@@ -1,0 +1,188 @@
+from contextlib import ExitStack
+
+import concourse.mybir as mybir
+from concourse.masks import make_identity
+
+TAPS, POINTS, CORNERS, COLUMNS, FEATURES, CHANNELS = 3, 256, 8, 2048, 1024, 128
+
+FLOPS = 2 * TAPS * FEATURES * POINTS * CHANNELS
+BYTES = 4 * FEATURES * COLUMNS + 4 * TAPS * FEATURES * CHANNELS + 4 * TAPS * POINTS * CORNERS + 2 * 128 * 384 + 4 * CHANNELS * POINTS
+
+F32 = mybir.dt.float32
+BF16 = mybir.dt.bfloat16
+U32 = mybir.dt.uint32
+U16 = mybir.dt.uint16
+U8 = mybir.dt.uint8
+FP8X4 = mybir.dt.float8_e4m3fn_x4
+COPY = mybir.ActivationFunctionType.Copy
+MULT = mybir.AluOpType.mult
+ADD = mybir.AluOpType.add
+
+P = 128
+HALVES = 2
+UNITS = TAPS * POINTS // P
+ENTRIES = P * CORNERS
+CHUNK = 512
+
+
+def tile_attend_deform_kernel(tc, xT, w, part, offs, out):
+    nc = tc.nc
+    with ExitStack() as ctx:
+        lists = ctx.enter_context(tc.tile_pool(name="lists", bufs=1))
+        keep = ctx.enter_context(tc.tile_pool(name="keep", bufs=1))
+        words_pool = ctx.enter_context(tc.tile_pool(name="words", bufs=4))
+        prod_pool = ctx.enter_context(tc.tile_pool(name="prod", bufs=3))
+        e_pool = ctx.enter_context(tc.tile_pool(name="epool", bufs=3))
+        lift_psum = ctx.enter_context(tc.psum_pool(name="lift", bufs=4))
+        sum_psum = ctx.enter_context(tc.psum_pool(name="sums", bufs=2))
+        acc_psum = ctx.enter_context(tc.psum_pool(name="accs", bufs=1))
+
+        offsets = lists.tile([P, TAPS * POINTS * CORNERS // 16], U16, name="offsets")
+
+        x_view = xT.rearrange("(s p u e) c -> s u p e c", s=HALVES, p=P, u=2, e=2)
+        raws = {}
+        tables = {}
+
+        def load_window(s, u):
+            for c in range(COLUMNS // CHUNK):
+                raw = keep.tile([P, 2, CHUNK], F32, name=f"raw{s}{u}{c}")
+                nc.sync.dma_start(raw[:], x_view[s, u, :, :, c * CHUNK : (c + 1) * CHUNK])
+                raws[s, u, c] = raw
+
+        def cast_window(s, u, engines):
+            table = keep.tile([P, COLUMNS, 2], BF16, name=f"table{s}{u}", align_bytes=64)
+            tables[s, u] = table
+            for c in range(COLUMNS // CHUNK):
+                dst = table[:, c * CHUNK : (c + 1) * CHUNK, :]
+                src = raws[s, u, c][:].rearrange("p e c -> p c e")
+                if engines[c] == "v":
+                    nc.vector.tensor_copy(dst, src)
+                else:
+                    nc.scalar.activation(dst, src, COPY)
+
+        load_window(0, 0)
+        nc.sync.dma_start(offsets[:], offs)
+        weights = keep.tile([P, UNITS, CORNERS], F32, name="weights")
+        nc.scalar.dma_start(weights[:], part[0:1, :].rearrange("one (k g j) -> g (one k) j", g=P, j=CORNERS))
+        load_window(0, 1)
+        w_raw = keep.tile([P, TAPS, HALVES, 4, CHANNELS], F32, name="w_raw")
+        w_view = w.rearrange("o (s p t) m -> o s p t m", s=HALVES, t=4)
+        for o in range(TAPS):
+            for s in range(HALVES):
+                nc.sync.dma_start(w_raw[:, o, s, :, :], w_view[o, s])
+        load_window(1, 0)
+        load_window(1, 1)
+
+        identity = keep.tile([P, P], F32, name="identity")
+        make_identity(nc, identity[:])
+
+        words = {}
+        prods = {}
+        sums = {}
+
+        def gather(s, k, u):
+            got = words_pool.tile([P, ENTRIES], U32, name=f"words{u}")
+            nc.vector.tensor_copy(
+                got[:].rearrange("p (q g h) -> p g h q", q=4, h=2),
+                tables[s, u][:].rearrange("p c e -> p (c e)").bitcast(U32).indirect(offsets[:, k * 64 : (k + 1) * 64]),
+            )
+            words[s, k, u] = got
+
+        def lift(s, k, b):
+            bank = lift_psum.tile([P, 2, 2, P], F32, name="bank")
+            for jj in range(2):
+                j = 2 * b + jj
+                h, q = j // 4, j % 4
+                for u in range(2):
+                    src = words[s, k, u][:, q * 256 : (q + 1) * 256].bitcast(F32).rearrange("p (g h) -> p g h", h=2)[:, :, h]
+                    nc.tensor.transpose(bank[:, jj, u, :], src, identity[:])
+            if b == 0:
+                prods[s, k] = prod_pool.tile([P, CORNERS, 512], F32, name="prod")
+            prod = prods[s, k]
+            for jj in range(2):
+                j = 2 * b + jj
+                nc.scalar.activation(
+                    prod[:, j, :].rearrange("p (u e m) -> p u e m", u=2, e=2),
+                    bank[:, jj, :, :].rearrange("p u m -> p (u m)").bitcast(BF16).rearrange("p (u m e) -> p u e m", u=2, e=2),
+                    COPY,
+                    scale=weights[:, k, j : j + 1],
+                )
+
+        def fold(s, k, t):
+            if t == 0:
+                sums[s, k] = sum_psum.tile([P, 4, P], F32, name="sum")
+            for j in range(CORNERS):
+                nc.tensor.matmul(
+                    sums[s, k][:, t, :],
+                    prods[s, k][:, j, t * P : (t + 1) * P],
+                    identity[:],
+                    start=(j == 0),
+                    stop=(j == CORNERS - 1),
+                    is_transpose=True,
+                )
+
+        w_codes = keep.tile([P, TAPS, HALVES, CHANNELS], U32, name="w_codes", align_bytes=64)
+        w_scales = keep.tile([P, TAPS, HALVES, CHANNELS], U8, name="w_scales", align_bytes=64)
+        w_bf = keep.tile([P, TAPS, HALVES, CHANNELS, 4], BF16, name="w_bf", align_bytes=64)
+
+        def quantize_w(o):
+            for s in range(HALVES):
+                nc.gpsimd.tensor_copy(w_bf[:, o, s, :, :], w_raw[:, o, s, :, :].rearrange("p t m -> p m t"))
+            nc.vector.quantize_mx(
+                out=w_codes[:, o, :, :].rearrange("p s m -> p (s m)").bitcast(FP8X4),
+                scales=w_scales[:, o, :, :].rearrange("p s m -> p (s m)"),
+                in_=w_bf[:, o, :, :, :].rearrange("p s m t -> p (s m t)"),
+            )
+
+        accs = [acc_psum.tile([P, P], F32, name=f"acc{b}") for b in range(2)]
+
+        def finish(s, k, i):
+            o, b = k // 2, k % 2
+            e_bf = e_pool.tile([P, P, 4], BF16, name="e_bf", align_bytes=64)
+            src = sums[s, k][:].rearrange("p t g -> p g t")
+            if i % 2 == 0:
+                nc.vector.tensor_copy(e_bf[:], src)
+            else:
+                nc.scalar.activation(e_bf[:], src, COPY)
+            codes = e_pool.tile([P, P], U32, name="codes", align_bytes=64)
+            scales = e_pool.tile([P, P], U8, name="scales", align_bytes=64)
+            nc.vector.quantize_mx(out=codes[:].bitcast(FP8X4), scales=scales[:], in_=e_bf[:].rearrange("p g t -> p (g t)"))
+            nc.tensor.matmul_mx(
+                out=accs[b][:],
+                lhsT=w_codes[:, o, s, :].bitcast(FP8X4),
+                lhsT_scale=w_scales[:, o, s, :],
+                rhs=codes[:].bitcast(FP8X4),
+                rhs_scale=scales[:],
+                start=(s == 0 and o == 0),
+                stop=(s == HALVES - 1 and o == TAPS - 1),
+            )
+            if s == HALVES - 1 and o == TAPS - 1:
+                result = e_pool.tile([P, P], F32, name="result")
+                nc.vector.tensor_copy(result[:], accs[b][:])
+                nc.sync.dma_start(out[:, b * P : (b + 1) * P], result[:])
+
+        units = [(s, k) for s in range(HALVES) for k in range(UNITS)]
+        cast_window(0, 0, "vvvv")
+        cast_window(0, 1, "ssss")
+        gather(0, 0, 0)
+        gather(0, 1, 0)
+        gather(0, 0, 1)
+        for i in range(len(units) + 1):
+            if i == 0:
+                gather(0, 1, 1)
+            elif i + 1 < len(units):
+                for u in range(2):
+                    gather(*units[i + 1], u)
+            if i == 1:
+                cast_window(1, 0, "vvvv")
+            if i == 2:
+                cast_window(1, 1, "vvvv")
+            if i < TAPS:
+                quantize_w(i)
+            for b in range(4):
+                if i < len(units):
+                    lift(*units[i], b)
+                if i > 0:
+                    fold(*units[i - 1], b)
+            if i > 0:
+                finish(*units[i - 1], i)

@@ -30,9 +30,9 @@ def tile_attend_deform_kernel(tc, xT, w, part, offs, out):
     with ExitStack() as ctx:
         lists = ctx.enter_context(tc.tile_pool(name="lists", bufs=1))
         keep = ctx.enter_context(tc.tile_pool(name="keep", bufs=1))
-        words_pool = ctx.enter_context(tc.tile_pool(name="words", bufs=4))
-        prod_pool = ctx.enter_context(tc.tile_pool(name="prod", bufs=3))
-        e_pool = ctx.enter_context(tc.tile_pool(name="epool", bufs=3))
+        words_pool = ctx.enter_context(tc.tile_pool(name="words", bufs=2))
+        prod_pool = ctx.enter_context(tc.tile_pool(name="prod", bufs=4))
+        e_pool = ctx.enter_context(tc.tile_pool(name="epool", bufs=4))
         lift_psum = ctx.enter_context(tc.psum_pool(name="lift", bufs=4))
         sum_psum = ctx.enter_context(tc.psum_pool(name="sums", bufs=2))
         acc_psum = ctx.enter_context(tc.psum_pool(name="accs", bufs=1))
@@ -45,7 +45,7 @@ def tile_attend_deform_kernel(tc, xT, w, part, offs, out):
 
         def load_window(s, u):
             for c in range(COLUMNS // CHUNK):
-                raw = keep.tile([P, 2, CHUNK], F32, name=f"raw{s}{u}{c}")
+                raw = keep.tile([P, 2, CHUNK], F32, name=f"raw{u}{c}")
                 nc.sync.dma_start(raw[:], x_view[s, u, :, :, c * CHUNK : (c + 1) * CHUNK])
                 raws[s, u, c] = raw
 
@@ -75,6 +75,8 @@ def tile_attend_deform_kernel(tc, xT, w, part, offs, out):
 
         identity = keep.tile([P, P], F32, name="identity")
         make_identity(nc, identity[:])
+        identity_bf = keep.tile([P, P], BF16, name="identity_bf")
+        make_identity(nc, identity_bf[:])
 
         words = {}
         prods = {}
@@ -83,27 +85,26 @@ def tile_attend_deform_kernel(tc, xT, w, part, offs, out):
         def gather(s, k, u):
             got = words_pool.tile([P, ENTRIES], U32, name=f"words{u}")
             nc.vector.tensor_copy(
-                got[:].rearrange("p (q g h) -> p g h q", q=4, h=2),
+                got[:],
                 tables[s, u][:].rearrange("p c e -> p (c e)").bitcast(U32).indirect(offsets[:, k * 64 : (k + 1) * 64]),
             )
             words[s, k, u] = got
 
         def lift(s, k, b):
-            bank = lift_psum.tile([P, 2, 2, P], F32, name="bank")
+            bank = lift_psum.tile([P, 2, 4, P], BF16, name="bank")
             for jj in range(2):
-                j = 2 * b + jj
-                h, q = j // 4, j % 4
-                for u in range(2):
-                    src = words[s, k, u][:, q * 256 : (q + 1) * 256].bitcast(F32).rearrange("p (g h) -> p g h", h=2)[:, :, h]
-                    nc.tensor.transpose(bank[:, jj, u, :], src, identity[:])
+                for t in range(4):
+                    u, e = t // 2, t % 2
+                    src = words[s, k, u][:].bitcast(BF16).rearrange("p (g x) -> p g x", g=P)[:, :, 2 * (2 * b + jj) + e]
+                    nc.tensor.transpose(bank[:, jj, t, :], src, identity_bf[:])
             if b == 0:
                 prods[s, k] = prod_pool.tile([P, CORNERS, 512], F32, name="prod")
             prod = prods[s, k]
             for jj in range(2):
                 j = 2 * b + jj
                 nc.scalar.activation(
-                    prod[:, j, :].rearrange("p (u e m) -> p u e m", u=2, e=2),
-                    bank[:, jj, :, :].rearrange("p u m -> p (u m)").bitcast(BF16).rearrange("p (u m e) -> p u e m", u=2, e=2),
+                    prod[:, j, :],
+                    bank[:, jj, :, :].rearrange("p t m -> p (t m)"),
                     COPY,
                     scale=weights[:, k, j : j + 1],
                 )
@@ -140,10 +141,7 @@ def tile_attend_deform_kernel(tc, xT, w, part, offs, out):
             o, b = k // 2, k % 2
             e_bf = e_pool.tile([P, P, 4], BF16, name="e_bf", align_bytes=64)
             src = sums[s, k][:].rearrange("p t g -> p g t")
-            if i % 2 == 0:
-                nc.vector.tensor_copy(e_bf[:], src)
-            else:
-                nc.scalar.activation(e_bf[:], src, COPY)
+            nc.scalar.activation(e_bf[:], src, COPY)
             codes = e_pool.tile([P, P], U32, name="codes", align_bytes=64)
             scales = e_pool.tile([P, P], U8, name="scales", align_bytes=64)
             nc.vector.quantize_mx(out=codes[:].bitcast(FP8X4), scales=scales[:], in_=e_bf[:].rearrange("p g t -> p (g t)"))
@@ -167,7 +165,9 @@ def tile_attend_deform_kernel(tc, xT, w, part, offs, out):
         gather(0, 0, 0)
         gather(0, 1, 0)
         gather(0, 0, 1)
-        for i in range(len(units) + 1):
+        for i in range(len(units) + 3):
+            if 0 <= i - 3:
+                finish(*units[i - 3], i)
             if i == 0:
                 gather(0, 1, 1)
             elif i + 1 < len(units):
@@ -182,7 +182,5 @@ def tile_attend_deform_kernel(tc, xT, w, part, offs, out):
             for b in range(4):
                 if i < len(units):
                     lift(*units[i], b)
-                if i > 0:
-                    fold(*units[i - 1], b)
-            if i > 0:
-                finish(*units[i - 1], i)
+                if 0 <= i - 2 < len(units):
+                    fold(*units[i - 2], b)

@@ -31,10 +31,10 @@ def tile_attend_deform_kernel(tc, xT, w, part, offs, out):
         lists = ctx.enter_context(tc.tile_pool(name="lists", bufs=1))
         keep = ctx.enter_context(tc.tile_pool(name="keep", bufs=1))
         words_pool = ctx.enter_context(tc.tile_pool(name="words", bufs=2))
-        prod_pool = ctx.enter_context(tc.tile_pool(name="prod", bufs=4))
+        prod_pool = ctx.enter_context(tc.tile_pool(name="prod", bufs=3))
         e_pool = ctx.enter_context(tc.tile_pool(name="epool", bufs=4))
         lift_psum = ctx.enter_context(tc.psum_pool(name="lift", bufs=4))
-        sum_psum = ctx.enter_context(tc.psum_pool(name="sums", bufs=2))
+        turn_psum = ctx.enter_context(tc.psum_pool(name="turn", bufs=2))
         acc_psum = ctx.enter_context(tc.psum_pool(name="accs", bufs=1))
 
         offsets = lists.tile([P, TAPS * POINTS * CORNERS // 16], U16, name="offsets")
@@ -45,7 +45,7 @@ def tile_attend_deform_kernel(tc, xT, w, part, offs, out):
 
         def load_window(s, u):
             for c in range(COLUMNS // CHUNK):
-                raw = keep.tile([P, 2, CHUNK], F32, name=f"raw{u}{c}")
+                raw = keep.tile([P, 2, CHUNK], F32, name=f"raw{s}{u}{c}")
                 nc.sync.dma_start(raw[:], x_view[s, u, :, :, c * CHUNK : (c + 1) * CHUNK])
                 raws[s, u, c] = raw
 
@@ -65,62 +65,55 @@ def tile_attend_deform_kernel(tc, xT, w, part, offs, out):
         weights = keep.tile([P, UNITS, CORNERS], F32, name="weights")
         nc.scalar.dma_start(weights[:], part[0:1, :].rearrange("one (k g j) -> g (one k) j", g=P, j=CORNERS))
         load_window(0, 1)
+        load_window(1, 0)
         w_raw = keep.tile([P, TAPS, HALVES, 4, CHANNELS], F32, name="w_raw")
         w_view = w.rearrange("o (s p t) m -> o s p t m", s=HALVES, t=4)
         for o in range(TAPS):
             for s in range(HALVES):
                 nc.sync.dma_start(w_raw[:, o, s, :, :], w_view[o, s])
-        load_window(1, 0)
         load_window(1, 1)
 
         identity = keep.tile([P, P], F32, name="identity")
         make_identity(nc, identity[:])
-        identity_bf = keep.tile([P, P], BF16, name="identity_bf")
-        make_identity(nc, identity_bf[:])
 
         words = {}
-        prods = {}
-        sums = {}
+        pairs = {}
 
         def gather(s, k, u):
             got = words_pool.tile([P, ENTRIES], U32, name=f"words{u}")
             nc.vector.tensor_copy(
-                got[:],
+                got[:].rearrange("p (q g h) -> p g q h", q=4, h=2),
                 tables[s, u][:].rearrange("p c e -> p (c e)").bitcast(U32).indirect(offsets[:, k * 64 : (k + 1) * 64]),
             )
             words[s, k, u] = got
 
-        def lift(s, k, b):
-            bank = lift_psum.tile([P, 2, 4, P], BF16, name="bank")
-            for jj in range(2):
-                for t in range(4):
-                    u, e = t // 2, t % 2
-                    src = words[s, k, u][:].bitcast(BF16).rearrange("p (g x) -> p g x", g=P)[:, :, 2 * (2 * b + jj) + e]
-                    nc.tensor.transpose(bank[:, jj, t, :], src, identity_bf[:])
-            if b == 0:
-                prods[s, k] = prod_pool.tile([P, CORNERS, 512], F32, name="prod")
-            prod = prods[s, k]
-            for jj in range(2):
-                j = 2 * b + jj
-                nc.scalar.activation(
-                    prod[:, j, :],
-                    bank[:, jj, :, :].rearrange("p t m -> p (t m)"),
-                    COPY,
-                    scale=weights[:, k, j : j + 1],
-                )
-
-        def fold(s, k, t):
-            if t == 0:
-                sums[s, k] = sum_psum.tile([P, 4, P], F32, name="sum")
-            for j in range(CORNERS):
-                nc.tensor.matmul(
-                    sums[s, k][:, t, :],
-                    prods[s, k][:, j, t * P : (t + 1) * P],
-                    identity[:],
-                    start=(j == 0),
-                    stop=(j == CORNERS - 1),
-                    is_transpose=True,
-                )
+        def corners(s, k, last):
+            prod = prod_pool.tile([P, CORNERS, 512], F32, name="prod")
+            pair = prod_pool.tile([P, 4, 512], F32, name="pair")
+            pairs[s, k] = pair
+            for q in (0, 2, 1, 3) if last else (0, 1, 2, 3):
+                bank = lift_psum.tile([P, 2, 2, P], F32, name="bank")
+                for h in range(2):
+                    for u in range(2):
+                        src = words[s, k, u][:].bitcast(F32).rearrange("p (q g h) -> p q g h", q=4, h=2)[:, q, :, h]
+                        nc.tensor.transpose(bank[:, h, u, :], src, identity[:])
+                for h in range(2):
+                    j = 2 * q + h
+                    src = bank[:, h, :, :].rearrange("p u m -> p (u m)").bitcast(BF16).rearrange("p (x e) -> p e x", e=2)
+                    scale = weights[:, k, j : j + 1]
+                    if last and j >= 4:
+                        nc.vector.scalar_tensor_tensor(
+                            pair[:, j - 4, :].rearrange("p (e x) -> p e x", e=2),
+                            src,
+                            scale,
+                            prod[:, j - 4, :].rearrange("p (e x) -> p e x", e=2),
+                            op0=MULT,
+                            op1=ADD,
+                        )
+                    else:
+                        nc.scalar.activation(prod[:, j, :].rearrange("p (e x) -> p e x", e=2), src, COPY, scale=scale)
+            if not last:
+                nc.gpsimd.tensor_tensor(pair[:], prod[:, 0:4, :], prod[:, 4:8, :], ADD)
 
         w_codes = keep.tile([P, TAPS, HALVES, CHANNELS], U32, name="w_codes", align_bytes=64)
         w_scales = keep.tile([P, TAPS, HALVES, CHANNELS], U8, name="w_scales", align_bytes=64)
@@ -137,11 +130,25 @@ def tile_attend_deform_kernel(tc, xT, w, part, offs, out):
 
         accs = [acc_psum.tile([P, P], F32, name=f"acc{b}") for b in range(2)]
 
-        def finish(s, k, i):
+        def finish(s, k, last):
             o, b = k // 2, k % 2
+            turned = turn_psum.tile([P, 4, P], F32, name="turned")
+            for t in range(4):
+                c = (t % 2 * 2 + t // 2) * P
+                for n in range(4):
+                    nc.tensor.matmul(
+                        turned[:, t, :],
+                        pairs[s, k][:, n, c : c + P],
+                        identity[:],
+                        start=(n == 0),
+                        stop=(n == 3),
+                        is_transpose=True,
+                    )
             e_bf = e_pool.tile([P, P, 4], BF16, name="e_bf", align_bytes=64)
-            src = sums[s, k][:].rearrange("p t g -> p g t")
-            nc.scalar.activation(e_bf[:], src, COPY)
+            if last:
+                nc.vector.tensor_copy(e_bf[:], turned[:].rearrange("p t g -> p g t"))
+            else:
+                nc.scalar.activation(e_bf[:], turned[:].rearrange("p t g -> p g t"), COPY)
             codes = e_pool.tile([P, P], U32, name="codes", align_bytes=64)
             scales = e_pool.tile([P, P], U8, name="scales", align_bytes=64)
             nc.vector.quantize_mx(out=codes[:].bitcast(FP8X4), scales=scales[:], in_=e_bf[:].rearrange("p g t -> p (g t)"))
@@ -160,27 +167,23 @@ def tile_attend_deform_kernel(tc, xT, w, part, offs, out):
                 nc.sync.dma_start(out[:, b * P : (b + 1) * P], result[:])
 
         units = [(s, k) for s in range(HALVES) for k in range(UNITS)]
+        final = len(units) - 1
         cast_window(0, 0, "vvvv")
         cast_window(0, 1, "ssss")
         gather(0, 0, 0)
         gather(0, 1, 0)
         gather(0, 0, 1)
-        for i in range(len(units) + 3):
-            if 0 <= i - 3:
-                finish(*units[i - 3], i)
+        for i in range(len(units) + 2):
             if i == 0:
                 gather(0, 1, 1)
-            elif i + 1 < len(units):
+            elif i < final:
                 for u in range(2):
                     gather(*units[i + 1], u)
-            if i == 1:
-                cast_window(1, 0, "vvvv")
-            if i == 2:
-                cast_window(1, 1, "vvvv")
+            if i <= final:
+                corners(*units[i], i == final)
+            if i in (1, 2):
+                cast_window(1, i - 1, "vvvv")
             if i < TAPS:
                 quantize_w(i)
-            for b in range(4):
-                if i < len(units):
-                    lift(*units[i], b)
-                if 0 <= i - 2 < len(units):
-                    fold(*units[i - 2], b)
+            if i >= 2:
+                finish(*units[i - 2], i - 2 == final)

@@ -30,9 +30,10 @@ def tile_attend_deform_kernel(tc, xT, w, part, offs, out):
     with ExitStack() as ctx:
         lists = ctx.enter_context(tc.tile_pool(name="lists", bufs=1))
         keep = ctx.enter_context(tc.tile_pool(name="keep", bufs=1))
-        words_pool = ctx.enter_context(tc.tile_pool(name="words", bufs=2))
-        prod_pool = ctx.enter_context(tc.tile_pool(name="prod", bufs=3))
-        e_pool = ctx.enter_context(tc.tile_pool(name="epool", bufs=4))
+        words_pool = ctx.enter_context(tc.tile_pool(name="words", bufs=3))
+        prod_pool = ctx.enter_context(tc.tile_pool(name="prod", bufs=5))
+        e_pool = ctx.enter_context(tc.tile_pool(name="epool", bufs=8))
+        code_pool = ctx.enter_context(tc.tile_pool(name="codes", bufs=4))
         lift_psum = ctx.enter_context(tc.psum_pool(name="lift", bufs=4))
         turn_psum = ctx.enter_context(tc.psum_pool(name="turn", bufs=2))
         acc_psum = ctx.enter_context(tc.psum_pool(name="accs", bufs=1))
@@ -49,16 +50,15 @@ def tile_attend_deform_kernel(tc, xT, w, part, offs, out):
                 nc.sync.dma_start(raw[:], x_view[s, u, :, :, c * CHUNK : (c + 1) * CHUNK])
                 raws[s, u, c] = raw
 
-        def cast_window(s, u, engines):
-            table = keep.tile([P, COLUMNS, 2], BF16, name=f"table{s}{u}", align_bytes=64)
-            tables[s, u] = table
-            for c in range(COLUMNS // CHUNK):
-                dst = table[:, c * CHUNK : (c + 1) * CHUNK, :]
-                src = raws[s, u, c][:].rearrange("p e c -> p c e")
-                if engines[c] == "v":
-                    nc.vector.tensor_copy(dst, src)
-                else:
-                    nc.scalar.activation(dst, src, COPY)
+        def cast_chunk(s, u, c, engine):
+            if c == 0:
+                tables[s, u] = keep.tile([P, COLUMNS, 2], BF16, name=f"table{s}{u}", align_bytes=64)
+            dst = tables[s, u][:, c * CHUNK : (c + 1) * CHUNK, :]
+            src = raws[s, u, c][:].rearrange("p e c -> p c e")
+            if engine == "v":
+                nc.vector.tensor_copy(dst, src)
+            else:
+                nc.scalar.activation(dst, src, COPY)
 
         load_window(0, 0)
         nc.sync.dma_start(offsets[:], offs)
@@ -76,44 +76,53 @@ def tile_attend_deform_kernel(tc, xT, w, part, offs, out):
         identity = keep.tile([P, P], F32, name="identity")
         make_identity(nc, identity[:])
 
+        units = [(s, u, k) for s in range(HALVES) for u in range(2) for k in range(UNITS)]
+        count = len(units)
         words = {}
-        pairs = {}
+        addends = {}
+        e_tiles = {}
 
-        def gather(s, k, u):
-            got = words_pool.tile([P, ENTRIES], U32, name=f"words{u}")
+        def gather(i):
+            s, u, k = units[i]
+            got = words_pool.tile([P, ENTRIES], U32, name="got")
             nc.vector.tensor_copy(
                 got[:].rearrange("p (q g h) -> p g q h", q=4, h=2),
                 tables[s, u][:].rearrange("p c e -> p (c e)").bitcast(U32).indirect(offsets[:, k * 64 : (k + 1) * 64]),
             )
-            words[s, k, u] = got
+            words[i] = got
 
-        def corners(s, k, last):
-            prod = prod_pool.tile([P, CORNERS, 512], F32, name="prod")
-            pair = prod_pool.tile([P, 4, 512], F32, name="pair")
-            pairs[s, k] = pair
-            for q in (0, 2, 1, 3) if last else (0, 1, 2, 3):
-                bank = lift_psum.tile([P, 2, 2, P], F32, name="bank")
-                for h in range(2):
-                    for u in range(2):
-                        src = words[s, k, u][:].bitcast(F32).rearrange("p (q g h) -> p q g h", q=4, h=2)[:, q, :, h]
-                        nc.tensor.transpose(bank[:, h, u, :], src, identity[:])
-                for h in range(2):
-                    j = 2 * q + h
-                    src = bank[:, h, :, :].rearrange("p u m -> p (u m)").bitcast(BF16).rearrange("p (x e) -> p e x", e=2)
+        def corners(i):
+            k = units[i][2]
+            late = i >= count - 2
+            prod = prod_pool.tile([P, CORNERS, 256], F32, name="prod")
+            pair = prod_pool.tile([P, 4, 256], F32, name="pair")
+            for b in range(2):
+                bank = lift_psum.tile([P, 4, P], F32, name="bank")
+                for jj in range(4):
+                    src = words[i][:].bitcast(F32).rearrange("p (q g h) -> p q g h", q=4, h=2)[:, 2 * b + jj // 2, :, jj % 2]
+                    nc.tensor.transpose(bank[:, jj, :], src, identity[:])
+                for jj in range(4):
+                    j = 4 * b + jj
+                    src = bank[:, jj, :].bitcast(BF16).rearrange("p (m e) -> p e m", e=2)
                     scale = weights[:, k, j : j + 1]
-                    if last and j >= 4:
+                    if late and b == 1:
                         nc.vector.scalar_tensor_tensor(
-                            pair[:, j - 4, :].rearrange("p (e x) -> p e x", e=2),
+                            pair[:, jj, :].rearrange("p (e m) -> p e m", e=2),
                             src,
                             scale,
-                            prod[:, j - 4, :].rearrange("p (e x) -> p e x", e=2),
+                            prod[:, jj, :].rearrange("p (e m) -> p e m", e=2),
                             op0=MULT,
                             op1=ADD,
                         )
                     else:
-                        nc.scalar.activation(prod[:, j, :].rearrange("p (e x) -> p e x", e=2), src, COPY, scale=scale)
-            if not last:
+                        nc.scalar.activation(prod[:, j, :].rearrange("p (e m) -> p e m", e=2), src, COPY, scale=scale)
+            if not late:
                 nc.gpsimd.tensor_tensor(pair[:], prod[:, 0:4, :], prod[:, 4:8, :], ADD)
+            addends[i] = [pair[:, n, :] for n in range(4)]
+            if i % 3 == 1 and i < 20:
+                both = prod_pool.tile([P, 2, 256], F32, name="both")
+                nc.gpsimd.tensor_tensor(both[:], pair[:, 0:2, :], pair[:, 2:4, :], ADD)
+                addends[i] = [both[:, n, :] for n in range(2)]
 
         w_codes = keep.tile([P, TAPS, HALVES, CHANNELS], U32, name="w_codes", align_bytes=64)
         w_scales = keep.tile([P, TAPS, HALVES, CHANNELS], U8, name="w_scales", align_bytes=64)
@@ -130,27 +139,33 @@ def tile_attend_deform_kernel(tc, xT, w, part, offs, out):
 
         accs = [acc_psum.tile([P, P], F32, name=f"acc{b}") for b in range(2)]
 
-        def finish(s, k, last):
+        def finish(i):
+            s, u, k = units[i]
             o, b = k // 2, k % 2
-            turned = turn_psum.tile([P, 4, P], F32, name="turned")
-            for t in range(4):
-                c = (t % 2 * 2 + t // 2) * P
-                for n in range(4):
+            turned = turn_psum.tile([P, 2, P], F32, name="turned")
+            for e in range(2):
+                for n, addend in enumerate(addends[i]):
                     nc.tensor.matmul(
-                        turned[:, t, :],
-                        pairs[s, k][:, n, c : c + P],
+                        turned[:, e, :],
+                        addend[:, e * P : (e + 1) * P],
                         identity[:],
                         start=(n == 0),
-                        stop=(n == 3),
+                        stop=(n == len(addends[i]) - 1),
                         is_transpose=True,
                     )
-            e_bf = e_pool.tile([P, P, 4], BF16, name="e_bf", align_bytes=64)
-            if last:
-                nc.vector.tensor_copy(e_bf[:], turned[:].rearrange("p t g -> p g t"))
+            if u == 0:
+                e_tiles[s, k] = e_pool.tile([P, P, 4], BF16, name="e_bf", align_bytes=64)
+            e_bf = e_tiles[s, k]
+            dst = e_bf[:, :, 2 * u : 2 * u + 2]
+            src = turned[:].rearrange("p e g -> p g e")
+            if i >= count - 2:
+                nc.vector.tensor_copy(dst, src)
             else:
-                nc.scalar.activation(e_bf[:], turned[:].rearrange("p t g -> p g t"), COPY)
-            codes = e_pool.tile([P, P], U32, name="codes", align_bytes=64)
-            scales = e_pool.tile([P, P], U8, name="scales", align_bytes=64)
+                nc.scalar.activation(dst, src, COPY)
+            if u == 0:
+                return
+            codes = code_pool.tile([P, P], U32, name="codes", align_bytes=64)
+            scales = code_pool.tile([P, P], U8, name="scales", align_bytes=64)
             nc.vector.quantize_mx(out=codes[:].bitcast(FP8X4), scales=scales[:], in_=e_bf[:].rearrange("p g t -> p (g t)"))
             nc.tensor.matmul_mx(
                 out=accs[b][:],
@@ -162,28 +177,22 @@ def tile_attend_deform_kernel(tc, xT, w, part, offs, out):
                 stop=(s == HALVES - 1 and o == TAPS - 1),
             )
             if s == HALVES - 1 and o == TAPS - 1:
-                result = e_pool.tile([P, P], F32, name="result")
+                result = code_pool.tile([P, P], F32, name="result")
                 nc.vector.tensor_copy(result[:], accs[b][:])
                 nc.sync.dma_start(out[:, b * P : (b + 1) * P], result[:])
 
-        units = [(s, k) for s in range(HALVES) for k in range(UNITS)]
-        final = len(units) - 1
-        cast_window(0, 0, "vvvv")
-        cast_window(0, 1, "ssss")
-        gather(0, 0, 0)
-        gather(0, 1, 0)
-        gather(0, 0, 1)
-        for i in range(len(units) + 2):
-            if i == 0:
-                gather(0, 1, 1)
-            elif i < final:
-                for u in range(2):
-                    gather(*units[i + 1], u)
-            if i <= final:
-                corners(*units[i], i == final)
-            if i in (1, 2):
-                cast_window(1, i - 1, "vvvv")
-            if i < TAPS:
-                quantize_w(i)
-            if i >= 2:
-                finish(*units[i - 2], i - 2 == final)
+        for c in range(4):
+            cast_chunk(0, 0, c, "v")
+        gather(0)
+        for i in range(count + 3):
+            if i + 1 < count:
+                gather(i + 1)
+            if i < count:
+                corners(i)
+            for first, s, u, engines in ((0, 0, 1, "svsv"), (1, 1, 0, "sssv"), (5, 1, 1, "ssss")):
+                if first <= i < first + 4:
+                    cast_chunk(s, u, i - first, engines[i - first])
+            if 5 <= i < 5 + TAPS:
+                quantize_w(i - 5)
+            if i >= 3:
+                finish(i - 3)

from contextlib import ExitStack

import concourse.mybir as mybir
from concourse.masks import make_identity

TAPS, POINTS, CORNERS, COLUMNS, FEATURES, CHANNELS = 3, 256, 8, 2048, 1024, 128

FLOPS = 2 * TAPS * FEATURES * POINTS * CHANNELS
BYTES = 4 * FEATURES * COLUMNS + 4 * TAPS * FEATURES * CHANNELS + 4 * TAPS * POINTS * CORNERS + 2 * 128 * 384 + 4 * CHANNELS * POINTS

F32 = mybir.dt.float32
BF16 = mybir.dt.bfloat16
U32 = mybir.dt.uint32
U16 = mybir.dt.uint16
U8 = mybir.dt.uint8
FP8X4 = mybir.dt.float8_e4m3fn_x4
COPY = mybir.ActivationFunctionType.Copy
MULT = mybir.AluOpType.mult
ADD = mybir.AluOpType.add

P = 128
HALVES = 2
UNITS = TAPS * POINTS // P
ENTRIES = P * CORNERS
CHUNK = 512


def tile_attend_deform_kernel(tc, xT, w, part, offs, out):
    nc = tc.nc
    with ExitStack() as ctx:
        lists = ctx.enter_context(tc.tile_pool(name="lists", bufs=1))
        keep = ctx.enter_context(tc.tile_pool(name="keep", bufs=1))
        words_pool = ctx.enter_context(tc.tile_pool(name="words", bufs=3))
        prod_pool = ctx.enter_context(tc.tile_pool(name="prod", bufs=5))
        e_pool = ctx.enter_context(tc.tile_pool(name="epool", bufs=8))
        code_pool = ctx.enter_context(tc.tile_pool(name="codes", bufs=4))
        lift_psum = ctx.enter_context(tc.psum_pool(name="lift", bufs=4))
        turn_psum = ctx.enter_context(tc.psum_pool(name="turn", bufs=2))
        acc_psum = ctx.enter_context(tc.psum_pool(name="accs", bufs=1))

        offsets = lists.tile([P, TAPS * POINTS * CORNERS // 16], U16, name="offsets")

        x_view = xT.rearrange("(s p u e) c -> s u p e c", s=HALVES, p=P, u=2, e=2)
        raws = {}
        tables = {}

        def load_window(s, u):
            for c in range(COLUMNS // CHUNK):
                raw = keep.tile([P, 2, CHUNK], F32, name=f"raw{s}{u}{c}")
                nc.sync.dma_start(raw[:], x_view[s, u, :, :, c * CHUNK : (c + 1) * CHUNK])
                raws[s, u, c] = raw

        def cast_chunk(s, u, c, engine):
            if c == 0:
                tables[s, u] = keep.tile([P, COLUMNS, 2], BF16, name=f"table{s}{u}", align_bytes=64)
            dst = tables[s, u][:, c * CHUNK : (c + 1) * CHUNK, :]
            src = raws[s, u, c][:].rearrange("p e c -> p c e")
            if engine == "v":
                nc.vector.tensor_copy(dst, src)
            else:
                nc.scalar.activation(dst, src, COPY)

        load_window(0, 0)
        nc.sync.dma_start(offsets[:], offs)
        weights = keep.tile([P, UNITS, CORNERS], F32, name="weights")
        nc.scalar.dma_start(weights[:], part[0:1, :].rearrange("one (k g j) -> g (one k) j", g=P, j=CORNERS))
        load_window(0, 1)
        load_window(1, 0)
        w_raw = keep.tile([P, TAPS, HALVES, 4, CHANNELS], F32, name="w_raw")
        w_view = w.rearrange("o (s p t) m -> o s p t m", s=HALVES, t=4)
        for o in range(TAPS):
            for s in range(HALVES):
                nc.sync.dma_start(w_raw[:, o, s, :, :], w_view[o, s])
        load_window(1, 1)

        identity = keep.tile([P, P], F32, name="identity")
        make_identity(nc, identity[:])

        units = [(s, u, k) for s in range(HALVES) for u in range(2) for k in range(UNITS)]
        count = len(units)
        words = {}
        addends = {}
        e_tiles = {}

        def gather(i):
            s, u, k = units[i]
            got = words_pool.tile([P, ENTRIES], U32, name="got")
            nc.vector.tensor_copy(
                got[:].rearrange("p (q g h) -> p g q h", q=4, h=2),
                tables[s, u][:].rearrange("p c e -> p (c e)").bitcast(U32).indirect(offsets[:, k * 64 : (k + 1) * 64]),
            )
            words[i] = got

        def corners(i):
            k = units[i][2]
            late = i >= count - 2
            prod = prod_pool.tile([P, CORNERS, 256], F32, name="prod")
            pair = prod_pool.tile([P, 4, 256], F32, name="pair")
            for b in range(2):
                bank = lift_psum.tile([P, 4, P], F32, name="bank")
                for jj in range(4):
                    src = words[i][:].bitcast(F32).rearrange("p (q g h) -> p q g h", q=4, h=2)[:, 2 * b + jj // 2, :, jj % 2]
                    nc.tensor.transpose(bank[:, jj, :], src, identity[:])
                for jj in range(4):
                    j = 4 * b + jj
                    src = bank[:, jj, :].bitcast(BF16).rearrange("p (m e) -> p e m", e=2)
                    scale = weights[:, k, j : j + 1]
                    if late and b == 1:
                        nc.vector.scalar_tensor_tensor(
                            pair[:, jj, :].rearrange("p (e m) -> p e m", e=2),
                            src,
                            scale,
                            prod[:, jj, :].rearrange("p (e m) -> p e m", e=2),
                            op0=MULT,
                            op1=ADD,
                        )
                    else:
                        nc.scalar.activation(prod[:, j, :].rearrange("p (e m) -> p e m", e=2), src, COPY, scale=scale)
            if not late:
                nc.gpsimd.tensor_tensor(pair[:], prod[:, 0:4, :], prod[:, 4:8, :], ADD)
            addends[i] = [pair[:, n, :] for n in range(4)]
            if i % 3 == 1 and i < 20:
                both = prod_pool.tile([P, 2, 256], F32, name="both")
                nc.gpsimd.tensor_tensor(both[:], pair[:, 0:2, :], pair[:, 2:4, :], ADD)
                addends[i] = [both[:, n, :] for n in range(2)]

        w_codes = keep.tile([P, TAPS, HALVES, CHANNELS], U32, name="w_codes", align_bytes=64)
        w_scales = keep.tile([P, TAPS, HALVES, CHANNELS], U8, name="w_scales", align_bytes=64)
        w_bf = keep.tile([P, TAPS, HALVES, CHANNELS, 4], BF16, name="w_bf", align_bytes=64)

        def quantize_w(o):
            for s in range(HALVES):
                nc.gpsimd.tensor_copy(w_bf[:, o, s, :, :], w_raw[:, o, s, :, :].rearrange("p t m -> p m t"))
            nc.vector.quantize_mx(
                out=w_codes[:, o, :, :].rearrange("p s m -> p (s m)").bitcast(FP8X4),
                scales=w_scales[:, o, :, :].rearrange("p s m -> p (s m)"),
                in_=w_bf[:, o, :, :, :].rearrange("p s m t -> p (s m t)"),
            )

        accs = [acc_psum.tile([P, P], F32, name=f"acc{b}") for b in range(2)]

        def finish(i):
            s, u, k = units[i]
            o, b = k // 2, k % 2
            turned = turn_psum.tile([P, 2, P], F32, name="turned")
            for e in range(2):
                for n, addend in enumerate(addends[i]):
                    nc.tensor.matmul(
                        turned[:, e, :],
                        addend[:, e * P : (e + 1) * P],
                        identity[:],
                        start=(n == 0),
                        stop=(n == len(addends[i]) - 1),
                        is_transpose=True,
                    )
            if u == 0:
                e_tiles[s, k] = e_pool.tile([P, P, 4], BF16, name="e_bf", align_bytes=64)
            e_bf = e_tiles[s, k]
            dst = e_bf[:, :, 2 * u : 2 * u + 2]
            src = turned[:].rearrange("p e g -> p g e")
            if i >= count - 2:
                nc.vector.tensor_copy(dst, src)
            else:
                nc.scalar.activation(dst, src, COPY)
            if u == 0:
                return
            codes = code_pool.tile([P, P], U32, name="codes", align_bytes=64)
            scales = code_pool.tile([P, P], U8, name="scales", align_bytes=64)
            nc.vector.quantize_mx(out=codes[:].bitcast(FP8X4), scales=scales[:], in_=e_bf[:].rearrange("p g t -> p (g t)"))
            nc.tensor.matmul_mx(
                out=accs[b][:],
                lhsT=w_codes[:, o, s, :].bitcast(FP8X4),
                lhsT_scale=w_scales[:, o, s, :],
                rhs=codes[:].bitcast(FP8X4),
                rhs_scale=scales[:],
                start=(s == 0 and o == 0),
                stop=(s == HALVES - 1 and o == TAPS - 1),
            )
            if s == HALVES - 1 and o == TAPS - 1:
                result = code_pool.tile([P, P], F32, name="result")
                nc.vector.tensor_copy(result[:], accs[b][:])
                nc.sync.dma_start(out[:, b * P : (b + 1) * P], result[:])

        for c in range(4):
            cast_chunk(0, 0, c, "v")
        gather(0)
        for i in range(count + 3):
            if i + 1 < count:
                gather(i + 1)
            if i < count:
                corners(i)
            for first, s, u, engines in ((0, 0, 1, "svsv"), (1, 1, 0, "sssv"), (5, 1, 1, "ssss")):
                if first <= i < first + 4:
                    cast_chunk(s, u, i - first, engines[i - first])
            if 5 <= i < 5 + TAPS:
                quantize_w(i - 5)
            if i >= 3:
                finish(i - 3)
